import numpy as np
import ml_dtypes


def mxq(x, axis, fmt="e4m3"):
    dtype, down = {"e4m3": (ml_dtypes.float8_e4m3fn, 7), "e5m2": (ml_dtypes.float8_e5m2, 14)}[fmt]
    v = np.moveaxis(np.asarray(x, np.float32).astype(ml_dtypes.bfloat16).astype(np.float64), axis, -1)
    blocks = v.reshape(v.shape[:-1] + (-1, 32))
    amax = np.abs(blocks).max(-1, keepdims=True)
    byte = np.maximum(np.where(amax > 0, np.frexp(amax)[1] - 1 + 127, 0) - down, 1)
    scale = np.exp2(byte - 127.0)
    codes = (blocks / scale).astype(np.float32).astype(dtype).astype(np.float64)
    return np.moveaxis((codes * scale).reshape(v.shape), -1, axis)


WIDE = False


def mx_kscale(k):
    if not WIDE:
        return np.ones(k)
    levels = np.array([10, -10, 5, -5, 0])
    if k % 512:
        return np.exp2(np.random.permutation(np.resize(levels, k // 32))).repeat(32)
    a = np.empty((k // 512, 16))
    for p in range(k // 512):
        a[p, :8] = np.random.permutation(np.resize(levels, 8))
        for g in range(8):
            far = levels[np.abs(levels - a[p, g]) >= 10]
            a[p, g + 8] = far[np.random.randint(len(far))]
    return np.exp2(a.ravel()).repeat(32)


def f64(x):
    return np.asarray(x).astype(np.float64)


def striped(idx):
    return np.tile(np.asarray(idx).reshape(-1, 16).T, (8, 1)).astype(np.uint16)


def unstriped(offs):
    return offs[:16].T.reshape(-1).astype(np.int64)


E2M1 = np.array([0.0, 0.5, 1.0, 1.5, 2.0, 3.0, 4.0, 6.0, -0.0, -0.5, -1.0, -1.5, -2.0, -3.0, -4.0, -6.0])


def pack_weight(w, fmt):
    k, n = w.shape
    w = f64(np.asarray(w, np.float32).astype(ml_dtypes.bfloat16)).reshape(k // 32, 32, n)
    amax = np.abs(w).max(1)
    if fmt == "e4m3":
        byte = np.frexp(amax)[1] - 1 + 127 - 7
    else:
        mant, ex = np.frexp(amax / 6.0)
        byte = np.where(mant > 0.5, ex, ex - 1) + 127
    byte = np.clip(np.where(amax > 0, byte, 1), 1, 254)
    scaled = (w * np.exp2(127.0 - byte)[:, None, :]).reshape(k, n).astype(np.float32)
    by_word = np.ascontiguousarray(scaled.reshape(k // 512, 128, 4, n).transpose(0, 1, 3, 2))
    if fmt == "e4m3":
        words = by_word.astype(ml_dtypes.float8_e4m3fn).view(np.uint8)
    else:
        c = by_word.astype(ml_dtypes.float4_e2m1fn).view(np.uint8) & 0xF
        words = (c[..., 0::2] | (c[..., 1::2] << 4)).reshape(k // 512, 128, 2 * n)
    return np.ascontiguousarray(words), np.ascontiguousarray(byte.astype(np.uint8).reshape(k // 512, 16, n))


def unpack_weight(words, scales, fmt):
    g, _, n = scales.shape
    words = np.ascontiguousarray(words).reshape(g, 128, n, -1)
    if fmt == "e4m3":
        vals = words.view(ml_dtypes.float8_e4m3fn).astype(np.float64)
    else:
        nib = np.empty((g, 128, n, 4), np.uint8)
        nib[..., 0::2] = words & 0xF
        nib[..., 1::2] = words >> 4
        vals = E2M1[nib]
    vals = vals * np.repeat(np.exp2(scales.astype(np.float64) - 127.0), 8, axis=1)[..., None]
    return vals.transpose(0, 1, 3, 2).reshape(g * 512, n)


def sigmoid(v):
    return 1.0 / (1.0 + np.exp(-v))


def rot(x):
    y = x.reshape(-1, 2, x.shape[1])
    return np.stack([-y[:, 1], y[:, 0]], axis=1).reshape(x.shape)


def bf(x):
    return np.asarray(x, np.float32).astype(ml_dtypes.bfloat16)


def planes(Y):
    r, m = Y.shape
    b = f64(bf(Y)).reshape(r // 32, 32, m)
    amax = np.abs(b).max(1)
    byte = np.clip(np.where(amax > 0, np.frexp(amax)[1] - 1 + 127 - 7, 1), 1, 254)
    codes = (b * np.exp2(127.0 - byte)[:, None, :]).reshape(r, m).astype(np.float32).astype(ml_dtypes.float8_e4m3fn).view(np.uint8)
    words = codes.reshape(r // 512, 128, 4, m).transpose(0, 1, 3, 2)
    return np.ascontiguousarray(words), np.ascontiguousarray(byte.astype(np.uint8).reshape(r // 512, 16, m))


K, R, F, T, J, U = 512, 512, 512, 2048, 256, 512


def setup_inputs():
    n = np.random.standard_normal
    idx = np.random.permutation(T)[:J]
    idx2 = np.random.randint(0, U, J)
    fk = mx_kscale(K)
    ff = mx_kscale(F)
    tabp = pack_weight(n((K, T)) / fk[:, None], "e4m3")
    return {
        "tab_words": tabp[0],
        "tab_scales": tabp[1],
        "w1": (n((K, R)) * 1 / np.sqrt(K) * fk[:, None]).astype(np.float32),
        "cosn": (np.repeat(np.round(np.cos(np.arange(R // 2)[:, None] * 0.11 + np.arange(U)[None] * 0.37) * 64) / 64, 2, axis=0)).astype(np.float32),
        "sinn": (np.repeat(np.round(np.sin(np.arange(R // 2)[:, None] * 0.11 + np.arange(U)[None] * 0.37) * 64) / 64, 2, axis=0)).astype(np.float32),
        "gain": (np.random.uniform(0.5, 1.5, (R, 1))).astype(np.float32),
        "wo": (n((F, R)) * 1 / np.sqrt(F) * ff[:, None]).astype(np.float32),
        "dy": (n((F, J)) / ff[:, None]).astype(np.float32),
        "old": (0.5 * n((R, J))).astype(np.float32),
        "offs": striped(idx),
        "offs2": striped(idx2),
    }


def reference(tab_words, tab_scales, w1, cosn, sinn, gain, wo, dy, old, offs, offs2):
    idx = unstriped(offs)
    idx2 = unstriped(offs2)
    tabu = unpack_weight(tab_words, tab_scales, "e4m3")
    w1q = mxq(f64(w1), 0, "e4m3")
    tabidxg = tabu[:, idx]
    a = w1q.T @ tabidxg
    o1 = rot(a)
    s = a * f64(cosn)[:, idx2] + o1 * f64(sinn)[:, idx2]
    s2 = s * f64(gain)
    woq = mxq(f64(wo), 0, "e4m3")
    dyq = mxq(f64(dy), 0, "e4m3")
    c0 = woq.T @ dyq
    ds2 = c0 * sigmoid(s2) * (1.0 + s2 * (1.0 - sigmoid(s2)))
    ds = ds2 * f64(gain)
    do1 = ds * f64(sinn)[:, idx2]
    odo1 = rot(do1)
    da = ds * f64(cosn)[:, idx2] - odo1
    y = da + f64(old)
    words, scales = planes(y)
    return y, words, scales

@@ -1,0 +1,177 @@
+from contextlib import ExitStack
+
+import concourse.mybir as mybir
+
+F32 = mybir.dt.float32
+BF16 = mybir.dt.bfloat16
+I32 = mybir.dt.int32
+U32 = mybir.dt.uint32
+U16 = mybir.dt.uint16
+U8 = mybir.dt.uint8
+FP8X4 = mybir.dt.float8_e4m3fn_x4
+ACT = mybir.ActivationFunctionType
+MULT = mybir.AluOpType.mult
+ADD = mybir.AluOpType.add
+SUB = mybir.AluOpType.subtract
+
+P = 128
+R, T, J, U = 512, 2048, 256, 512
+H = 128
+FLOPS = 2 * 2 * 512 * 512 * 256
+BYTES = 5 * 2**20 + 32768 + 2048 + 8192 + 2**19 + 2**17 + 4096
+
+
+def tile_attend_cturned_pl_kernel(tc, tab_words, tab_scales, w1, cosn, sinn, gain, wo, dy, old, offs, offs2, out_0, out_1, out_2):
+    nc = tc.nc
+    with ExitStack() as ctx:
+        sb = ctx.enter_context(tc.tile_pool(name="sb", bufs=1))
+        ps = ctx.enter_context(tc.psum_pool(name="ps", bufs=1))
+
+        def tile(name, shape, dtype):
+            return sb.tile(shape, dtype, name=name, align_bytes=64)
+
+        slots = tile("slots", [P, J // 16], U16)
+        angles = tile("angles", [P, J // 16], U16)
+        w1_raw = tile("w1_raw", [P, 4, R], F32)
+        wo_raw = tile("wo_raw", [P, 4, R], F32)
+        dy_raw = tile("dy_raw", [P, 4, J], F32)
+        old_sb = tile("old_sb", [P, 4, J], F32)
+        cos_tab = tile("cos_tab", [P, 2, U], F32)
+        sin_tab = tile("sin_tab", [P, 2, U], F32)
+        gains = tile("gains", [P, 4], F32)
+        words = tile("words", [P, T], I32)
+        scale_tab = tile("scale_tab", [P, T], U8)
+
+        warm = tile("warm", [P, 2], F32)
+        nc.vector.memset(warm[:, 0:1], 0.0)
+        nc.scalar.activation(warm[:, 1:2], warm[:, 0:1], ACT.Silu)
+
+        nc.vector.memset(scale_tab[:].bitcast(I32), 0)
+        nc.sync.dma_start(out=w1_raw[:], in_=w1.rearrange("(p j) c -> p j c", j=4))
+        for q in range(4):
+            nc.sync.dma_start(out=scale_tab[32 * q : 32 * q + 4, :].bitcast(I32), in_=tab_scales[0][4 * q : 4 * q + 4, :].bitcast(I32))
+        nc.sync.dma_start(angles[:], offs2)
+        nc.sync.dma_start(out=gains[:], in_=gain.rearrange("(p t) o -> p (t o)", t=4))
+        nc.sync.dma_start(out=cos_tab[:], in_=cosn.rearrange("(p e two) u -> p e two u", e=2, two=2)[:, :, 0, :])
+        nc.sync.dma_start(out=sin_tab[:], in_=sinn.rearrange("(p e two) u -> p e two u", e=2, two=2)[:, :, 0, :])
+        nc.sync.dma_start(slots[:], offs)
+        nc.sync.dma_start(out=words[:], in_=tab_words[0].rearrange("p c b -> p (c b)").bitcast(I32))
+        nc.sync.dma_start(out=dy_raw[:], in_=dy.rearrange("(p j) c -> p j c", j=4))
+        nc.sync.dma_start(out=wo_raw[:], in_=wo.rearrange("(p j) c -> p j c", j=4))
+        nc.sync.dma_start(out=old_sb[:], in_=old.rearrange("(p t) c -> p t c", t=4))
+
+        def deal(engine_copy, dst, raw, m0, m1):
+            engine_copy(dst[:].rearrange("p (t m j) -> p m t j", t=4, j=4)[:, m0:m1],
+                        raw[:].rearrange("p j (m t) -> p m t j", t=4)[:, m0:m1])
+
+        def weave(engine_copy, dst, src):
+            engine_copy(dst.rearrange("p (c i t) -> p c t i", i=4, t=4), src.rearrange("p t (c i) -> p c t i", i=4))
+
+        def quantise(name, src, width):
+            codes = tile(name + "_codes", [P, width], U32)
+            scales = tile(name + "_scales", [P, width], U8)
+            nc.vector.quantize_mx(out=codes[:].bitcast(FP8X4), scales=scales[:], in_=src[:])
+            return codes, scales
+
+        w1_bf = tile("w1_bf", [P, 4 * R], BF16)
+        deal(nc.vector.tensor_copy, w1_bf, w1_raw, 0, 80)
+        deal(nc.scalar.copy, w1_bf, w1_raw, 80, 128)
+        w1_codes, w1_scales = quantise("w1", w1_bf, R)
+
+        signed = tile("signed", [P, 4], F32)
+        gv = gains[:].rearrange("p (e two) -> p e two", two=2)
+        sv = signed[:].rearrange("p (e two) -> p e two", two=2)
+        nc.vector.tensor_scalar(sv[:, :, 0], gv[:, :, 0], -1.0, None, MULT)
+        nc.vector.tensor_copy(sv[:, :, 1], gv[:, :, 1])
+
+        cos_g = tile("cos_g", [P, 4, J], F32)
+        sin_g = tile("sin_g", [P, 4, J], F32)
+        for name, tab, factor, dst in (("cos", cos_tab, gains, cos_g), ("sin", sin_tab, signed, sin_g)):
+            for e in range(2):
+                picked = tile("%s_picked%d" % (name, e), [P, J], F32)
+                nc.vector.tensor_copy(picked[:], tab[:, e, :].indirect(angles[:]))
+                for t in (2 * e, 2 * e + 1):
+                    nc.scalar.activation(dst[:, t, :], picked[:], ACT.Copy, scale=factor[:, t : t + 1])
+
+        tab_scale_g = tile("tab_scale_g", [P, J], U8)
+        nc.vector.tensor_copy(tab_scale_g[:], scale_tab[:].indirect(slots[:]))
+        tab_g = tile("tab_g", [P, J], U32)
+        nc.vector.tensor_copy(tab_g[:], words[:].bitcast(U32).indirect(slots[:]))
+
+        def product(name, h, lhs_codes, lhs_scales, rhs_codes, rhs_scales):
+            bank = ps.tile([P, 4, H], F32, name="%s%d" % (name, h))
+            cols = slice(h * H, (h + 1) * H)
+            for t in range(4):
+                nc.tensor.matmul_mx(out=bank[:, t, :], lhsT=lhs_codes[:, t * P : (t + 1) * P].bitcast(FP8X4), lhsT_scale=lhs_scales[:, t * P : (t + 1) * P],
+                                    rhs=rhs_codes[:, cols].bitcast(FP8X4), rhs_scale=rhs_scales[:, cols], start=True, stop=True)
+            return bank
+
+        def pairs(ap):
+            return ap.rearrange("p (e two) j -> p e two j", two=2)
+
+        a = [product("a", h, w1_codes, w1_scales, tab_g, tab_scale_g) for h in range(2)]
+
+        dy_bf = tile("dy_bf", [P, 4 * J], BF16)
+        weave(nc.scalar.copy, dy_bf[:], dy_raw[:])
+
+        def turn(h):
+            cols = slice(h * H, (h + 1) * H)
+            u = tile("u%d" % h, [P, 4, H], F32)
+            v = tile("v%d" % h, [P, 4, H], F32)
+            s2 = tile("s2_%d" % h, [P, 4, H], F32)
+            nc.vector.tensor_tensor(u[:], a[h][:], cos_g[:, :, cols], MULT)
+            for two in range(2):
+                nc.vector.tensor_tensor(pairs(v[:])[:, :, two, :], pairs(a[h][:])[:, :, 1 - two, :], pairs(sin_g[:, :, cols])[:, :, two, :], MULT)
+            nc.vector.tensor_tensor(s2[:], u[:], v[:], ADD)
+            return s2
+
+        def activate(h, s2):
+            th = tile("th%d" % h, [P, 4, H], F32)
+            ns = tile("ns%d" % h, [P, 4, H], F32)
+            nc.scalar.activation(th[:], s2[:], ACT.Tanh, scale=0.5)
+            nc.scalar.activation(ns[:], s2[:], ACT.Silu, scale=-1.0)
+            return th, ns
+
+        s2_first = turn(0)
+        dy_codes, dy_scales = quantise("dy", dy_bf, J)
+        wo_bf = tile("wo_bf", [P, 4 * R], BF16)
+        deal(nc.vector.tensor_copy, wo_bf, wo_raw, 0, 64)
+        deal(nc.scalar.copy, wo_bf, wo_raw, 64, 128)
+        wo_codes, wo_scales = quantise("wo", wo_bf, R)
+        c0 = [product("c0", h, wo_codes, wo_scales, dy_codes, dy_scales) for h in range(2)]
+        acts = [activate(0, s2_first), activate(1, turn(1))]
+        half_tanh = [x[0] for x in acts]
+        neg_silu = [x[1] for x in acts]
+
+        out_rows = out_0.rearrange("(p t) c -> p t c", t=4)
+        out_words = out_1[0].rearrange("p c b -> p (c b)").bitcast(I32)
+        out_scales = out_2[0].bitcast(I32)
+        y_scales = tile("y_scales", [P, J], U8)
+        for h in range(2):
+            cols = slice(h * H, (h + 1) * H)
+            q = tile("q%d" % h, [P, 4, H], F32)
+            ds = tile("ds%d" % h, [P, 4, H], F32)
+            m1 = tile("m1_%d" % h, [P, 4, H], F32)
+            m2 = tile("m2_%d" % h, [P, 4, H], F32)
+            da = tile("da%d" % h, [P, 4, H], F32)
+            y = tile("y%d" % h, [P, 4, H], F32)
+            nc.vector.scalar_tensor_tensor(q[:], half_tanh[h][:], 1.0, c0[h][:], ADD, MULT)
+            nc.vector.scalar_tensor_tensor(ds[:], neg_silu[h][:], 1.0, q[:], SUB, MULT)
+            nc.vector.tensor_tensor(m1[:], ds[:], cos_g[:, :, cols], MULT)
+            for two in range(2):
+                nc.vector.tensor_tensor(pairs(m2[:])[:, :, two, :], pairs(ds[:])[:, :, 1 - two, :], pairs(sin_g[:, :, cols])[:, :, 1 - two, :], MULT)
+            nc.vector.tensor_tensor(da[:], m1[:], m2[:], ADD)
+            nc.vector.scalar_tensor_tensor(y[:], da[:], -0.5, old_sb[:, :, cols], MULT, ADD)
+            nc.sync.dma_start(out=out_rows[:, :, cols], in_=y[:])
+            y_bf = tile("y_bf%d" % h, [P, 4 * H], BF16)
+            if h == 0:
+                weave(nc.scalar.copy, y_bf[:], y[:])
+            else:
+                weave(nc.vector.tensor_copy, y_bf[:, : 4 * 80], y[:, :, :80])
+                weave(nc.scalar.copy, y_bf[:, 4 * 80 :], y[:, :, 80:])
+            y_codes = tile("y_codes%d" % h, [P, H], U32)
+            nc.vector.quantize_mx(out=y_codes[:].bitcast(FP8X4), scales=y_scales[:, cols], in_=y_bf[:])
+            nc.sync.dma_start(out=out_words[:, cols], in_=y_codes[:].bitcast(I32))
+        for q in range(4):
+            engine = nc.sync if q % 2 == 0 else nc.scalar
+            engine.dma_start(out=out_scales[4 * q : 4 * q + 4, :], in_=y_scales[32 * q : 32 * q + 4, :].bitcast(I32))

@@ -1,6 +1,7 @@
 from contextlib import ExitStack
 
 import concourse.mybir as mybir
+from concourse.masks import make_identity
 
 F32 = mybir.dt.float32
 BF16 = mybir.dt.bfloat16
@@ -37,7 +38,7 @@ def tile_attend_cturned_pl_kernel(tc, tab_words, tab_scales, w1, cosn, sinn, gai
         dy_raw = tile("dy_raw", [P, 4, J], F32)
         old_sb = tile("old_sb", [P, 4, J], F32)
         cos_tab = tile("cos_tab", [P, 2, U], F32)
-        sin_tab = tile("sin_tab", [P, 2, U], F32)
+        sin_tab = [tile("sin_tab%d" % e, [P, U], F32) for e in range(2)]
         gains = tile("gains", [P, 4], F32)
         words = tile("words", [P, T], I32)
         scale_tab = tile("scale_tab", [P, T], U8)
@@ -46,18 +47,23 @@ def tile_attend_cturned_pl_kernel(tc, tab_words, tab_scales, w1, cosn, sinn, gai
         nc.vector.memset(warm[:, 0:1], 0.0)
         nc.scalar.activation(warm[:, 1:2], warm[:, 0:1], ACT.Silu)
 
-        nc.vector.memset(scale_tab[:].bitcast(I32), 0)
-        nc.sync.dma_start(out=w1_raw[:], in_=w1.rearrange("(p j) c -> p j c", j=4))
-        for q in range(4):
-            nc.sync.dma_start(out=scale_tab[32 * q : 32 * q + 4, :].bitcast(I32), in_=tab_scales[0][4 * q : 4 * q + 4, :].bitcast(I32))
+        nc.gpsimd.memset(scale_tab[:].bitcast(I32), 0)
+        identity = tile("identity", [P, P], F32)
+        make_identity(nc, identity[:])
+        cos_rows = cosn.rearrange("(p e two) u -> p e two u", e=2, two=2)[:, :, 0, :]
+        sin_rows = sinn.rearrange("(p e two) u -> p e two u", e=2, two=2)[:, :, 0, :]
         nc.sync.dma_start(angles[:], offs2)
-        nc.sync.dma_start(out=gains[:], in_=gain.rearrange("(p t) o -> p (t o)", t=4))
-        nc.sync.dma_start(out=cos_tab[:], in_=cosn.rearrange("(p e two) u -> p e two u", e=2, two=2)[:, :, 0, :])
-        nc.sync.dma_start(out=sin_tab[:], in_=sinn.rearrange("(p e two) u -> p e two u", e=2, two=2)[:, :, 0, :])
+        nc.scalar.dma_start(out=gains[:], in_=gain.rearrange("(p t) o -> p (t o)", t=4))
+        nc.sync.dma_start(out=cos_tab[:], in_=cos_rows)
+        nc.sync.dma_start(out=w1_raw[:], in_=w1.rearrange("(p j) c -> p j c", j=4))
+        for q4 in range(4):
+            nc.sync.dma_start(out=scale_tab[32 * q4 : 32 * q4 + 4, :].bitcast(I32), in_=tab_scales[0][4 * q4 : 4 * q4 + 4, :].bitcast(I32))
         nc.sync.dma_start(slots[:], offs)
+        nc.sync.dma_start(out=sin_tab[0][:], in_=sin_rows[:, 0, :])
         nc.sync.dma_start(out=words[:], in_=tab_words[0].rearrange("p c b -> p (c b)").bitcast(I32))
-        nc.sync.dma_start(out=dy_raw[:], in_=dy.rearrange("(p j) c -> p j c", j=4))
+        nc.sync.dma_start(out=sin_tab[1][:], in_=sin_rows[:, 1, :])
         nc.sync.dma_start(out=wo_raw[:], in_=wo.rearrange("(p j) c -> p j c", j=4))
+        nc.sync.dma_start(out=dy_raw[:], in_=dy.rearrange("(p j) c -> p j c", j=4))
         nc.sync.dma_start(out=old_sb[:], in_=old.rearrange("(p t) c -> p t c", t=4))
 
         def deal(engine_copy, dst, raw, m0, m1):
@@ -86,17 +92,21 @@ def tile_attend_cturned_pl_kernel(tc, tab_words, tab_scales, w1, cosn, sinn, gai
 
         cos_g = tile("cos_g", [P, 4, J], F32)
         sin_g = tile("sin_g", [P, 4, J], F32)
-        for name, tab, factor, dst in (("cos", cos_tab, gains, cos_g), ("sin", sin_tab, signed, sin_g)):
-            for e in range(2):
-                picked = tile("%s_picked%d" % (name, e), [P, J], F32)
-                nc.vector.tensor_copy(picked[:], tab[:, e, :].indirect(angles[:]))
-                for t in (2 * e, 2 * e + 1):
-                    nc.scalar.activation(dst[:, t, :], picked[:], ACT.Copy, scale=factor[:, t : t + 1])
 
+        def look_up(name, window, factor, dst, e, flip):
+            picked = tile("%s_picked%d" % (name, e), [P, J], F32)
+            nc.vector.tensor_copy(picked[:], window.indirect(angles[:]))
+            for t in (2 * e, 2 * e + 1):
+                nc.scalar.activation(dst[:, t ^ flip, :], picked[:], ACT.Copy, scale=factor[:, t : t + 1])
+
+        look_up("cos", cos_tab[:, 0, :], gains, cos_g, 0, 0)
+        look_up("cos", cos_tab[:, 1, :], gains, cos_g, 1, 0)
+        look_up("sin", sin_tab[0][:], signed, sin_g, 0, 1)
         tab_scale_g = tile("tab_scale_g", [P, J], U8)
         nc.vector.tensor_copy(tab_scale_g[:], scale_tab[:].indirect(slots[:]))
         tab_g = tile("tab_g", [P, J], U32)
         nc.vector.tensor_copy(tab_g[:], words[:].bitcast(U32).indirect(slots[:]))
+        look_up("sin", sin_tab[1][:], signed, sin_g, 1, 1)
 
         def product(name, h, lhs_codes, lhs_scales, rhs_codes, rhs_scales):
             bank = ps.tile([P, 4, H], F32, name="%s%d" % (name, h))
@@ -106,42 +116,71 @@ def tile_attend_cturned_pl_kernel(tc, tab_words, tab_scales, w1, cosn, sinn, gai
                                     rhs=rhs_codes[:, cols].bitcast(FP8X4), rhs_scale=rhs_scales[:, cols], start=True, stop=True)
             return bank
 
-        def pairs(ap):
-            return ap.rearrange("p (e two) j -> p e two j", two=2)
+        def turned_sum(bank, first, second):
+            for t in range(4):
+                nc.tensor.matmul(bank[:, t, :], first[:, t, :], identity[:], start=(t == 0), stop=False, is_transpose=True)
+            for t in range(4):
+                nc.tensor.matmul(bank[:, t, :], second[:, t ^ 1, :], identity[:], start=False, stop=(t == 3), is_transpose=True)
 
         a = [product("a", h, w1_codes, w1_scales, tab_g, tab_scale_g) for h in range(2)]
 
-        dy_bf = tile("dy_bf", [P, 4 * J], BF16)
-        weave(nc.scalar.copy, dy_bf[:], dy_raw[:])
+        def both(name):
+            return [tile("%s%d" % (name, h), [P, 4, H], F32) for h in range(2)]
 
-        def turn(h):
+        halves = [slice(h * H, (h + 1) * H) for h in range(2)]
+        u, v = both("u"), both("v")
+        for h in range(2):
+            nc.vector.tensor_tensor(u[h][:], a[h][:], cos_g[:, :, halves[h]], MULT)
+        s2 = []
+        for h in range(2):
+            nc.vector.tensor_tensor(v[h][:], a[h][:], sin_g[:, :, halves[h]], MULT)
+            bank = ps.tile([P, 4, H], F32, name="sum%d" % h)
+            turned_sum(bank, u[h], v[h])
+            s2.append(bank)
+
+        cos_t, sin_t = [], []
+        for h in range(2):
             cols = slice(h * H, (h + 1) * H)
-            u = tile("u%d" % h, [P, 4, H], F32)
-            v = tile("v%d" % h, [P, 4, H], F32)
-            s2 = tile("s2_%d" % h, [P, 4, H], F32)
-            nc.vector.tensor_tensor(u[:], a[h][:], cos_g[:, :, cols], MULT)
-            for two in range(2):
-                nc.vector.tensor_tensor(pairs(v[:])[:, :, two, :], pairs(a[h][:])[:, :, 1 - two, :], pairs(sin_g[:, :, cols])[:, :, two, :], MULT)
-            nc.vector.tensor_tensor(s2[:], u[:], v[:], ADD)
-            return s2
+            cb = ps.tile([P, 4, H], F32, name="cos_t%d" % h)
+            sn = ps.tile([P, 4, H], F32, name="sin_t%d" % h)
+            for t in range(4):
+                nc.tensor.transpose(cb[:, t, :], cos_g[:, t, cols], identity[:])
+            for t in range(4):
+                nc.tensor.transpose(sn[:, t, :], sin_g[:, t ^ 1, cols], identity[:])
+            cos_t.append(cb)
+            sin_t.append(sn)
 
-        def activate(h, s2):
-            th = tile("th%d" % h, [P, 4, H], F32)
-            ns = tile("ns%d" % h, [P, 4, H], F32)
-            nc.scalar.activation(th[:], s2[:], ACT.Tanh, scale=0.5)
-            nc.scalar.activation(ns[:], s2[:], ACT.Silu, scale=-1.0)
-            return th, ns
-
-        s2_first = turn(0)
-        dy_codes, dy_scales = quantise("dy", dy_bf, J)
         wo_bf = tile("wo_bf", [P, 4 * R], BF16)
-        deal(nc.vector.tensor_copy, wo_bf, wo_raw, 0, 64)
-        deal(nc.scalar.copy, wo_bf, wo_raw, 64, 128)
+        weave(nc.scalar.copy, wo_bf[:], wo_raw[:])
         wo_codes, wo_scales = quantise("wo", wo_bf, R)
-        c0 = [product("c0", h, wo_codes, wo_scales, dy_codes, dy_scales) for h in range(2)]
-        acts = [activate(0, s2_first), activate(1, turn(1))]
-        half_tanh = [x[0] for x in acts]
-        neg_silu = [x[1] for x in acts]
+        c0 = []
+        for h in range(2):
+            dy_bf = tile("dy_bf%d" % h, [P, 4 * H], BF16)
+            weave(nc.vector.tensor_copy, dy_bf[:], dy_raw[:, :, halves[h]])
+            dy_codes, dy_scales = quantise("dy%d" % h, dy_bf, H)
+            bank = ps.tile([P, 4, H], F32, name="a%d" % h)
+            flat = bank[:].rearrange("j t p -> j (t p)")
+            nc.tensor.matmul_mx(out=flat, lhsT=dy_codes[:].bitcast(FP8X4), lhsT_scale=dy_scales[:],
+                                rhs=wo_codes[:].bitcast(FP8X4), rhs_scale=wo_scales[:], start=True, stop=True)
+            c0.append(flat.rearrange("j (p t) -> j t p", t=4))
+
+        th, ns, q, ds, m1, m2, y = [both(n) for n in ("th", "ns", "q", "ds", "m1_", "m2_", "y")]
+        for h in range(2):
+            nc.scalar.activation(th[h][:], s2[h][:], ACT.Tanh, scale=0.5)
+        for h in range(2):
+            nc.scalar.activation(ns[h][:], s2[h][:], ACT.Silu, scale=-1.0)
+        for h in range(2):
+            nc.vector.scalar_tensor_tensor(q[h][:], th[h][:], 1.0, c0[h], ADD, MULT)
+        for h in range(2):
+            nc.vector.scalar_tensor_tensor(ds[h][:], ns[h][:], 1.0, q[h][:], SUB, MULT)
+        da = []
+        for h in range(2):
+            nc.vector.tensor_tensor(m1[h][:], ds[h][:], cos_t[h][:], MULT)
+            for part in ([slice(0, 4)] if h == 0 else [slice(0, 2), slice(2, 4)]):
+                nc.vector.tensor_tensor(m2[h][:, part, :], ds[h][:, part, :], sin_t[h][:, part, :], MULT)
+            bank = ps.tile([P, 4, H], F32, name="sum%d" % h)
+            turned_sum(bank, m1[h], m2[h])
+            da.append(bank)
 
         out_rows = out_0.rearrange("(p t) c -> p t c", t=4)
         out_words = out_1[0].rearrange("p c b -> p (c b)").bitcast(I32)
@@ -149,29 +188,17 @@ def tile_attend_cturned_pl_kernel(tc, tab_words, tab_scales, w1, cosn, sinn, gai
         y_scales = tile("y_scales", [P, J], U8)
         for h in range(2):
             cols = slice(h * H, (h + 1) * H)
-            q = tile("q%d" % h, [P, 4, H], F32)
-            ds = tile("ds%d" % h, [P, 4, H], F32)
-            m1 = tile("m1_%d" % h, [P, 4, H], F32)
-            m2 = tile("m2_%d" % h, [P, 4, H], F32)
-            da = tile("da%d" % h, [P, 4, H], F32)
-            y = tile("y%d" % h, [P, 4, H], F32)
-            nc.vector.scalar_tensor_tensor(q[:], half_tanh[h][:], 1.0, c0[h][:], ADD, MULT)
-            nc.vector.scalar_tensor_tensor(ds[:], neg_silu[h][:], 1.0, q[:], SUB, MULT)
-            nc.vector.tensor_tensor(m1[:], ds[:], cos_g[:, :, cols], MULT)
-            for two in range(2):
-                nc.vector.tensor_tensor(pairs(m2[:])[:, :, two, :], pairs(ds[:])[:, :, 1 - two, :], pairs(sin_g[:, :, cols])[:, :, 1 - two, :], MULT)
-            nc.vector.tensor_tensor(da[:], m1[:], m2[:], ADD)
-            nc.vector.scalar_tensor_tensor(y[:], da[:], -0.5, old_sb[:, :, cols], MULT, ADD)
-            nc.sync.dma_start(out=out_rows[:, :, cols], in_=y[:])
+            nc.vector.scalar_tensor_tensor(y[h][:], da[h][:], -0.5, old_sb[:, :, cols], MULT, ADD)
+            nc.sync.dma_start(out=out_rows[:, :, cols], in_=y[h][:])
             y_bf = tile("y_bf%d" % h, [P, 4 * H], BF16)
             if h == 0:
-                weave(nc.scalar.copy, y_bf[:], y[:])
+                weave(nc.scalar.copy, y_bf[:], y[h][:])
             else:
-                weave(nc.vector.tensor_copy, y_bf[:, : 4 * 80], y[:, :, :80])
-                weave(nc.scalar.copy, y_bf[:, 4 * 80 :], y[:, :, 80:])
+                weave(nc.vector.tensor_copy, y_bf[:, : 4 * 80], y[h][:, :, :80])
+                weave(nc.scalar.copy, y_bf[:, 4 * 80 :], y[h][:, :, 80:])
             y_codes = tile("y_codes%d" % h, [P, H], U32)
             nc.vector.quantize_mx(out=y_codes[:].bitcast(FP8X4), scales=y_scales[:, cols], in_=y_bf[:])
             nc.sync.dma_start(out=out_words[:, cols], in_=y_codes[:].bitcast(I32))
-        for q in range(4):
-            engine = nc.sync if q % 2 == 0 else nc.scalar
-            engine.dma_start(out=out_scales[4 * q : 4 * q + 4, :], in_=y_scales[32 * q : 32 * q + 4, :].bitcast(I32))
+        for q4 in range(4):
+            engine = nc.sync if q4 % 2 == 0 else nc.scalar
+            engine.dma_start(out=out_scales[4 * q4 : 4 * q4 + 4, :], in_=y_scales[32 * q4 : 32 * q4 + 4, :].bitcast(I32))

@@ -18,6 +18,7 @@ SUB = mybir.AluOpType.subtract
 P = 128
 R, T, J, U = 512, 2048, 256, 512
 H = 128
+WO_SPLIT = 96
 FLOPS = 2 * 2 * 512 * 512 * 256
 BYTES = 5 * 2**20 + 32768 + 2048 + 8192 + 2**19 + 2**17 + 4096
 
@@ -28,8 +29,8 @@ def tile_attend_cturned_pl_kernel(tc, tab_words, tab_scales, w1, cosn, sinn, gai
         sb = ctx.enter_context(tc.tile_pool(name="sb", bufs=1))
         ps = ctx.enter_context(tc.psum_pool(name="ps", bufs=1))
 
-        def tile(name, shape, dtype):
-            return sb.tile(shape, dtype, name=name, align_bytes=64)
+        def tile(name, shape, dtype, tag=None):
+            return sb.tile(shape, dtype, name=name, tag=tag or name, align_bytes=64)
 
         slots = tile("slots", [P, J // 16], U16)
         angles = tile("angles", [P, J // 16], U16)
@@ -57,7 +58,7 @@ def tile_attend_cturned_pl_kernel(tc, tab_words, tab_scales, w1, cosn, sinn, gai
         nc.sync.dma_start(out=cos_tab[:], in_=cos_rows)
         nc.sync.dma_start(out=w1_raw[:], in_=w1.rearrange("(p j) c -> p j c", j=4))
         for q4 in range(4):
-            nc.sync.dma_start(out=scale_tab[32 * q4 : 32 * q4 + 4, :].bitcast(I32), in_=tab_scales[0][4 * q4 : 4 * q4 + 4, :].bitcast(I32))
+            nc.sync.dma_start(out=scale_tab[q4:P:32, :].bitcast(I32), in_=tab_scales[0][q4:16:4, :].bitcast(I32))
         nc.sync.dma_start(slots[:], offs)
         nc.sync.dma_start(out=sin_tab[0][:], in_=sin_rows[:, 0, :])
         nc.sync.dma_start(out=words[:], in_=tab_words[0].rearrange("p c b -> p (c b)").bitcast(I32))
@@ -76,13 +77,8 @@ def tile_attend_cturned_pl_kernel(tc, tab_words, tab_scales, w1, cosn, sinn, gai
         def quantise(name, src, width):
             codes = tile(name + "_codes", [P, width], U32)
             scales = tile(name + "_scales", [P, width], U8)
-            nc.vector.quantize_mx(out=codes[:].bitcast(FP8X4), scales=scales[:], in_=src[:])
+            nc.vector.quantize_mx(out=codes[:].bitcast(FP8X4), scales=scales[:], in_=src)
             return codes, scales
-
-        w1_bf = tile("w1_bf", [P, 4 * R], BF16)
-        deal(nc.vector.tensor_copy, w1_bf, w1_raw, 0, 80)
-        deal(nc.scalar.copy, w1_bf, w1_raw, 80, 128)
-        w1_codes, w1_scales = quantise("w1", w1_bf, R)
 
         signed = tile("signed", [P, 4], F32)
         gv = gains[:].rearrange("p (e two) -> p e two", two=2)
@@ -101,6 +97,11 @@ def tile_attend_cturned_pl_kernel(tc, tab_words, tab_scales, w1, cosn, sinn, gai
 
         look_up("cos", cos_tab[:, 0, :], gains, cos_g, 0, 0)
         look_up("cos", cos_tab[:, 1, :], gains, cos_g, 1, 0)
+        w1_bf = tile("w1_bf", [P, 4 * R], BF16)
+        deal(nc.vector.tensor_copy, w1_bf, w1_raw, 0, 80)
+        deal(nc.scalar.copy, w1_bf, w1_raw, 80, 128)
+        w1_codes, w1_scales = quantise("w1", w1_bf[:], R)
+
         look_up("sin", sin_tab[0][:], signed, sin_g, 0, 1)
         tab_scale_g = tile("tab_scale_g", [P, J], U8)
         nc.vector.tensor_copy(tab_scale_g[:], scale_tab[:].indirect(slots[:]))
@@ -138,31 +139,34 @@ def tile_attend_cturned_pl_kernel(tc, tab_words, tab_scales, w1, cosn, sinn, gai
             turned_sum(bank, u[h], v[h])
             s2.append(bank)
 
+        wo_bf = tile("wo_bf", [P, 4 * R], BF16, tag="sin_picked1")
+        weave(nc.vector.tensor_copy, wo_bf[:, : 4 * WO_SPLIT], wo_raw[:, :, :WO_SPLIT])
+        weave(nc.scalar.copy, wo_bf[:, 4 * WO_SPLIT :], wo_raw[:, :, WO_SPLIT:])
+        c0 = []
+        dy_both = tile("dy_bf", [P, 2, 4 * H], BF16, tag="w1_codes")
+        for h in range(2):
+            dy_bf = dy_both[:, h, :]
+            weave(nc.vector.tensor_copy, dy_bf, dy_raw[:, :, halves[h]])
+            if h == 0:
+                wo_codes, wo_scales = quantise("wo", wo_bf[:], R)
+            dy_codes, dy_scales = quantise("dy%d" % h, dy_bf, H)
+            bank = ps.tile([P, 4, H], F32, name="c%d" % h)
+            flat = bank[:].rearrange("j t p -> j (t p)")
+            nc.tensor.matmul_mx(out=flat, lhsT=dy_codes[:].bitcast(FP8X4), lhsT_scale=dy_scales[:],
+                                rhs=wo_codes[:].bitcast(FP8X4), rhs_scale=wo_scales[:], start=True, stop=True)
+            c0.append(flat.rearrange("j (p t) -> j t p", t=4))
+
         cos_t, sin_t = [], []
         for h in range(2):
             cols = slice(h * H, (h + 1) * H)
             cb = ps.tile([P, 4, H], F32, name="cos_t%d" % h)
-            sn = ps.tile([P, 4, H], F32, name="sin_t%d" % h)
+            sn = ps.tile([P, 4, H], F32, name="a%d" % h)
             for t in range(4):
                 nc.tensor.transpose(cb[:, t, :], cos_g[:, t, cols], identity[:])
             for t in range(4):
                 nc.tensor.transpose(sn[:, t, :], sin_g[:, t ^ 1, cols], identity[:])
             cos_t.append(cb)
             sin_t.append(sn)
-
-        wo_bf = tile("wo_bf", [P, 4 * R], BF16)
-        weave(nc.scalar.copy, wo_bf[:], wo_raw[:])
-        wo_codes, wo_scales = quantise("wo", wo_bf, R)
-        c0 = []
-        for h in range(2):
-            dy_bf = tile("dy_bf%d" % h, [P, 4 * H], BF16)
-            weave(nc.vector.tensor_copy, dy_bf[:], dy_raw[:, :, halves[h]])
-            dy_codes, dy_scales = quantise("dy%d" % h, dy_bf, H)
-            bank = ps.tile([P, 4, H], F32, name="a%d" % h)
-            flat = bank[:].rearrange("j t p -> j (t p)")
-            nc.tensor.matmul_mx(out=flat, lhsT=dy_codes[:].bitcast(FP8X4), lhsT_scale=dy_scales[:],
-                                rhs=wo_codes[:].bitcast(FP8X4), rhs_scale=wo_scales[:], start=True, stop=True)
-            c0.append(flat.rearrange("j (p t) -> j t p", t=4))
 
         th, ns, q, ds, m1, m2, y = [both(n) for n in ("th", "ns", "q", "ds", "m1_", "m2_", "y")]
         for h in range(2):

from contextlib import ExitStack

import concourse.mybir as mybir
from concourse.masks import make_identity

F32 = mybir.dt.float32
BF16 = mybir.dt.bfloat16
I32 = mybir.dt.int32
U32 = mybir.dt.uint32
U16 = mybir.dt.uint16
U8 = mybir.dt.uint8
FP8X4 = mybir.dt.float8_e4m3fn_x4
ACT = mybir.ActivationFunctionType
MULT = mybir.AluOpType.mult
ADD = mybir.AluOpType.add
SUB = mybir.AluOpType.subtract

P = 128
R, T, J, U = 512, 2048, 256, 512
H = 128
WO_SPLIT = 96
FLOPS = 2 * 2 * 512 * 512 * 256
BYTES = 5 * 2**20 + 32768 + 2048 + 8192 + 2**19 + 2**17 + 4096


def tile_attend_cturned_pl_kernel(tc, tab_words, tab_scales, w1, cosn, sinn, gain, wo, dy, old, offs, offs2, out_0, out_1, out_2):
    nc = tc.nc
    with ExitStack() as ctx:
        sb = ctx.enter_context(tc.tile_pool(name="sb", bufs=1))
        ps = ctx.enter_context(tc.psum_pool(name="ps", bufs=1))

        def tile(name, shape, dtype, tag=None):
            return sb.tile(shape, dtype, name=name, tag=tag or name, align_bytes=64)

        slots = tile("slots", [P, J // 16], U16)
        angles = tile("angles", [P, J // 16], U16)
        w1_raw = tile("w1_raw", [P, 4, R], F32)
        wo_raw = tile("wo_raw", [P, 4, R], F32)
        dy_raw = tile("dy_raw", [P, 4, J], F32)
        old_sb = tile("old_sb", [P, 4, J], F32)
        cos_tab = tile("cos_tab", [P, 2, U], F32)
        sin_tab = [tile("sin_tab%d" % e, [P, U], F32) for e in range(2)]
        gains = tile("gains", [P, 4], F32)
        words = tile("words", [P, T], I32)
        scale_tab = tile("scale_tab", [P, T], U8)

        warm = tile("warm", [P, 2], F32)
        nc.vector.memset(warm[:, 0:1], 0.0)
        nc.scalar.activation(warm[:, 1:2], warm[:, 0:1], ACT.Silu)

        nc.gpsimd.memset(scale_tab[:].bitcast(I32), 0)
        identity = tile("identity", [P, P], F32)
        make_identity(nc, identity[:])
        cos_rows = cosn.rearrange("(p e two) u -> p e two u", e=2, two=2)[:, :, 0, :]
        sin_rows = sinn.rearrange("(p e two) u -> p e two u", e=2, two=2)[:, :, 0, :]
        nc.sync.dma_start(angles[:], offs2)
        nc.scalar.dma_start(out=gains[:], in_=gain.rearrange("(p t) o -> p (t o)", t=4))
        nc.sync.dma_start(out=cos_tab[:], in_=cos_rows)
        nc.sync.dma_start(out=w1_raw[:], in_=w1.rearrange("(p j) c -> p j c", j=4))
        for q4 in range(4):
            nc.sync.dma_start(out=scale_tab[q4:P:32, :].bitcast(I32), in_=tab_scales[0][q4:16:4, :].bitcast(I32))
        nc.sync.dma_start(slots[:], offs)
        nc.sync.dma_start(out=sin_tab[0][:], in_=sin_rows[:, 0, :])
        nc.sync.dma_start(out=words[:], in_=tab_words[0].rearrange("p c b -> p (c b)").bitcast(I32))
        nc.sync.dma_start(out=sin_tab[1][:], in_=sin_rows[:, 1, :])
        nc.sync.dma_start(out=wo_raw[:], in_=wo.rearrange("(p j) c -> p j c", j=4))
        nc.sync.dma_start(out=dy_raw[:], in_=dy.rearrange("(p j) c -> p j c", j=4))
        nc.sync.dma_start(out=old_sb[:], in_=old.rearrange("(p t) c -> p t c", t=4))

        def deal(engine_copy, dst, raw, m0, m1):
            engine_copy(dst[:].rearrange("p (t m j) -> p m t j", t=4, j=4)[:, m0:m1],
                        raw[:].rearrange("p j (m t) -> p m t j", t=4)[:, m0:m1])

        def weave(engine_copy, dst, src):
            engine_copy(dst.rearrange("p (c i t) -> p c t i", i=4, t=4), src.rearrange("p t (c i) -> p c t i", i=4))

        def quantise(name, src, width):
            codes = tile(name + "_codes", [P, width], U32)
            scales = tile(name + "_scales", [P, width], U8)
            nc.vector.quantize_mx(out=codes[:].bitcast(FP8X4), scales=scales[:], in_=src)
            return codes, scales

        signed = tile("signed", [P, 4], F32)
        gv = gains[:].rearrange("p (e two) -> p e two", two=2)
        sv = signed[:].rearrange("p (e two) -> p e two", two=2)
        nc.vector.tensor_scalar(sv[:, :, 0], gv[:, :, 0], -1.0, None, MULT)
        nc.vector.tensor_copy(sv[:, :, 1], gv[:, :, 1])

        cos_g = tile("cos_g", [P, 4, J], F32)
        sin_g = tile("sin_g", [P, 4, J], F32)

        def look_up(name, window, factor, dst, e, flip):
            picked = tile("%s_picked%d" % (name, e), [P, J], F32)
            nc.vector.tensor_copy(picked[:], window.indirect(angles[:]))
            for t in (2 * e, 2 * e + 1):
                nc.scalar.activation(dst[:, t ^ flip, :], picked[:], ACT.Copy, scale=factor[:, t : t + 1])

        look_up("cos", cos_tab[:, 0, :], gains, cos_g, 0, 0)
        look_up("cos", cos_tab[:, 1, :], gains, cos_g, 1, 0)
        w1_bf = tile("w1_bf", [P, 4 * R], BF16)
        deal(nc.vector.tensor_copy, w1_bf, w1_raw, 0, 80)
        deal(nc.scalar.copy, w1_bf, w1_raw, 80, 128)
        w1_codes, w1_scales = quantise("w1", w1_bf[:], R)

        look_up("sin", sin_tab[0][:], signed, sin_g, 0, 1)
        tab_scale_g = tile("tab_scale_g", [P, J], U8)
        nc.vector.tensor_copy(tab_scale_g[:], scale_tab[:].indirect(slots[:]))
        tab_g = tile("tab_g", [P, J], U32)
        nc.vector.tensor_copy(tab_g[:], words[:].bitcast(U32).indirect(slots[:]))
        look_up("sin", sin_tab[1][:], signed, sin_g, 1, 1)

        def product(name, h, lhs_codes, lhs_scales, rhs_codes, rhs_scales):
            bank = ps.tile([P, 4, H], F32, name="%s%d" % (name, h))
            cols = slice(h * H, (h + 1) * H)
            for t in range(4):
                nc.tensor.matmul_mx(out=bank[:, t, :], lhsT=lhs_codes[:, t * P : (t + 1) * P].bitcast(FP8X4), lhsT_scale=lhs_scales[:, t * P : (t + 1) * P],
                                    rhs=rhs_codes[:, cols].bitcast(FP8X4), rhs_scale=rhs_scales[:, cols], start=True, stop=True)
            return bank

        def turned_sum(bank, first, second):
            for t in range(4):
                nc.tensor.matmul(bank[:, t, :], first[:, t, :], identity[:], start=(t == 0), stop=False, is_transpose=True)
            for t in range(4):
                nc.tensor.matmul(bank[:, t, :], second[:, t ^ 1, :], identity[:], start=False, stop=(t == 3), is_transpose=True)

        a = [product("a", h, w1_codes, w1_scales, tab_g, tab_scale_g) for h in range(2)]

        def both(name):
            return [tile("%s%d" % (name, h), [P, 4, H], F32) for h in range(2)]

        halves = [slice(h * H, (h + 1) * H) for h in range(2)]
        u, v = both("u"), both("v")
        for h in range(2):
            nc.vector.tensor_tensor(u[h][:], a[h][:], cos_g[:, :, halves[h]], MULT)
        s2 = []
        for h in range(2):
            nc.vector.tensor_tensor(v[h][:], a[h][:], sin_g[:, :, halves[h]], MULT)
            bank = ps.tile([P, 4, H], F32, name="sum%d" % h)
            turned_sum(bank, u[h], v[h])
            s2.append(bank)

        wo_bf = tile("wo_bf", [P, 4 * R], BF16, tag="sin_picked1")
        weave(nc.vector.tensor_copy, wo_bf[:, : 4 * WO_SPLIT], wo_raw[:, :, :WO_SPLIT])
        weave(nc.scalar.copy, wo_bf[:, 4 * WO_SPLIT :], wo_raw[:, :, WO_SPLIT:])
        c0 = []
        dy_both = tile("dy_bf", [P, 2, 4 * H], BF16, tag="w1_codes")
        for h in range(2):
            dy_bf = dy_both[:, h, :]
            weave(nc.vector.tensor_copy, dy_bf, dy_raw[:, :, halves[h]])
            if h == 0:
                wo_codes, wo_scales = quantise("wo", wo_bf[:], R)
            dy_codes, dy_scales = quantise("dy%d" % h, dy_bf, H)
            bank = ps.tile([P, 4, H], F32, name="c%d" % h)
            flat = bank[:].rearrange("j t p -> j (t p)")
            nc.tensor.matmul_mx(out=flat, lhsT=dy_codes[:].bitcast(FP8X4), lhsT_scale=dy_scales[:],
                                rhs=wo_codes[:].bitcast(FP8X4), rhs_scale=wo_scales[:], start=True, stop=True)
            c0.append(flat.rearrange("j (p t) -> j t p", t=4))

        cos_t, sin_t = [], []
        for h in range(2):
            cols = slice(h * H, (h + 1) * H)
            cb = ps.tile([P, 4, H], F32, name="cos_t%d" % h)
            sn = ps.tile([P, 4, H], F32, name="a%d" % h)
            for t in range(4):
                nc.tensor.transpose(cb[:, t, :], cos_g[:, t, cols], identity[:])
            for t in range(4):
                nc.tensor.transpose(sn[:, t, :], sin_g[:, t ^ 1, cols], identity[:])
            cos_t.append(cb)
            sin_t.append(sn)

        th, ns, q, ds, m1, m2, y = [both(n) for n in ("th", "ns", "q", "ds", "m1_", "m2_", "y")]
        for h in range(2):
            nc.scalar.activation(th[h][:], s2[h][:], ACT.Tanh, scale=0.5)
        for h in range(2):
            nc.scalar.activation(ns[h][:], s2[h][:], ACT.Silu, scale=-1.0)
        for h in range(2):
            nc.vector.scalar_tensor_tensor(q[h][:], th[h][:], 1.0, c0[h], ADD, MULT)
        for h in range(2):
            nc.vector.scalar_tensor_tensor(ds[h][:], ns[h][:], 1.0, q[h][:], SUB, MULT)
        da = []
        for h in range(2):
            nc.vector.tensor_tensor(m1[h][:], ds[h][:], cos_t[h][:], MULT)
            for part in ([slice(0, 4)] if h == 0 else [slice(0, 2), slice(2, 4)]):
                nc.vector.tensor_tensor(m2[h][:, part, :], ds[h][:, part, :], sin_t[h][:, part, :], MULT)
            bank = ps.tile([P, 4, H], F32, name="sum%d" % h)
            turned_sum(bank, m1[h], m2[h])
            da.append(bank)

        out_rows = out_0.rearrange("(p t) c -> p t c", t=4)
        out_words = out_1[0].rearrange("p c b -> p (c b)").bitcast(I32)
        out_scales = out_2[0].bitcast(I32)
        y_scales = tile("y_scales", [P, J], U8)
        for h in range(2):
            cols = slice(h * H, (h + 1) * H)
            nc.vector.scalar_tensor_tensor(y[h][:], da[h][:], -0.5, old_sb[:, :, cols], MULT, ADD)
            nc.sync.dma_start(out=out_rows[:, :, cols], in_=y[h][:])
            y_bf = tile("y_bf%d" % h, [P, 4 * H], BF16)
            if h == 0:
                weave(nc.scalar.copy, y_bf[:], y[h][:])
            else:
                weave(nc.vector.tensor_copy, y_bf[:, : 4 * 80], y[h][:, :, :80])
                weave(nc.scalar.copy, y_bf[:, 4 * 80 :], y[h][:, :, 80:])
            y_codes = tile("y_codes%d" % h, [P, H], U32)
            nc.vector.quantize_mx(out=y_codes[:].bitcast(FP8X4), scales=y_scales[:, cols], in_=y_bf[:])
            nc.sync.dma_start(out=out_words[:, cols], in_=y_codes[:].bitcast(I32))
        for q4 in range(4):
            engine = nc.sync if q4 % 2 == 0 else nc.scalar
            engine.dma_start(out=out_scales[4 * q4 : 4 * q4 + 4, :], in_=y_scales[32 * q4 : 32 * q4 + 4, :].bitcast(I32))
